import numpy as np, ml_dtypes
CORES = [242,247,114,119]
N = 4
KB, QP = 1, 256
def setup_inputs(rng):
    q = rng.standard_normal((N, 128, QP), dtype=np.float32) / 4; k = rng.standard_normal((N, 128, KB * 128), dtype=np.float32)
    a = 2 * np.pi * rng.random((N, QP)); s = 400 * rng.random((N, QP)) ** 1.5; q[:, 0, :] = s * np.cos(a); q[:, 1, :] = s * np.sin(a); q[:, 2, :] = 150 * rng.standard_normal((N, QP)); k[:, 2, :] = 1 + k[:, 2, :] / 50
    a = (2 * np.pi * rng.random() + np.pi / 2 * (rng.permutation(N).reshape(N, 1, 1) + 0.5) / N - 0.5 + (np.arange(KB).reshape(1, KB, 1) + rng.random((N, KB, 128))) / KB).reshape(N, KB * 128); k[:, 0, :] = np.cos(a); k[:, 1, :] = np.sin(a)
    return {"q": q.astype(ml_dtypes.bfloat16), "k": k.astype(ml_dtypes.bfloat16), "v": rng.standard_normal((N, 128, KB * 128), dtype=np.float32).astype(ml_dtypes.bfloat16)}
def setup_inputs_big(rng):
    d = setup_inputs(rng)
    for k in ("v",): d[k] = (d[k].astype(np.float32) * 1048576.0).astype(d[k].dtype)
    return d
def setup_inputs_small(rng):
    d = setup_inputs(rng)
    for k in ("v",): d[k] = (d[k].astype(np.float32) * (1 / 1048576.0)).astype(d[k].dtype)
    return d
def reference(q, k, v):
    Q, K, V = q.astype(np.float64), k.astype(np.float64), v.astype(np.float64)
    y = np.zeros((N, QP, 128))
    for r in range(N):
        js = list(range(N))
        S = np.concatenate([K[j].T @ Q[r] for j in js], axis=0)
        P = np.exp(S - S.max(axis=0)); P = P / P.sum(axis=0)
        y[r] = P.T @ np.concatenate([V[j][:, 128 * b:128 * b + 128] for j in js for b in range(KB)], axis=0)
    return {"y": y.astype(ml_dtypes.bfloat16)}

@@ -1,0 +1,225 @@
+from concourse.bass import DstId, RemoteDMATransfer
+from concourse.mybir import AluOpType, AxisListType, ActivationFunctionType
+
+N = 4
+QB = 2
+SIZES = (1, 1, 2)
+NL = len(SIZES)
+FIRST = tuple(sum(SIZES[:i]) for i in range(NL))
+
+SCRATCH = {
+    "kv": ("sbuf", [128, N * 256], "bfloat16"),
+    "qs": ("sbuf", [128, QB * 128], "bfloat16"),
+    "ident": ("sbuf", [128, 128], "bfloat16"),
+    "p": ("sbuf", [128, QB * N * 128], "bfloat16"),
+    "pt": ("sbuf", [128, QB * N * 128], "bfloat16"),
+    "df": ("sbuf", [128, NL * QB * 128], "bfloat16"),
+    "op": ("sbuf", [128, NL * QB * 128], "bfloat16"),
+    "negm": ("sbuf", [128, NL * QB], "float32"),
+    "lsum": ("sbuf", [128, NL * QB], "float32"),
+    "fcol": ("sbuf", [128, NL * QB], "float32"),
+    "lrun": ("sbuf", [128, NL * QB], "float32"),
+    "rinv": ("sbuf", [128, QB], "float32"),
+    "ys": ("sbuf", [128, QB * 128], "bfloat16"),
+    "st00": ("psum", [128, 512], "float32"), "st01": ("psum", [128, 512], "float32"),
+    "st10": ("psum", [128, 512], "float32"), "st11": ("psum", [128, 512], "float32"),
+    "tp0": ("psum", [128, 1024], "bfloat16"), "tp1": ("psum", [128, 1024], "bfloat16"),
+    "yp0": ("psum", [128, 512], "float32"), "yp1": ("psum", [128, 512], "float32"),
+}
+
+SEMAPHORES = ["ones", "idn", "ldk", "ldv", "ldq", "sent", "rc", "out", "ny0", "ny1"] + ["arr%d" % j for j in range(N)]
+for _g in range(NL):
+    for _b in range(QB):
+        _names = ["st", "red", "ex", "tr", "cp", "pv"]
+        if _g > 0:
+            _names += ["put", "f", "df", "l"]
+        if _g < NL - 1:
+            _names += ["oc"]
+        SEMAPHORES += ["%s%d%d" % (_n, _g, _b) for _n in _names]
+
+
+def _bits(m):
+    return bin(m).count("1")
+
+
+def rank_program(g, core, T, topo):
+    rank = T.rank_of(core)
+    if rank is None:
+        return
+    cores = T.cores
+    te, ve, ac, sy = g.tensor, g.vector, g.scalar, g.sync
+    Exp, Copy = ActivationFunctionType.Exp, ActivationFunctionType.Copy
+    mult, add, amax = AluOpType.mult, AluOpType.add, AluOpType.max
+
+    def S(name, lv, b):
+        return T.sem["%s%d%d" % (name, lv, b)]
+
+    def plan(r):
+        c = cores[r]
+        here = lambda j: topo.host(cores[j]) == topo.host(c) and topo.chip(cores[j]) == topo.chip(c)
+        near = [j for j in range(N) if j != r and here(j)]
+        far = [j for j in range(N) if j != r and not here(j)]
+        far.sort(key=lambda j: topo.die(cores[j]) != topo.die(c))
+        m_far = topo.mask(c, cores[far[0]])
+        for j in far:
+            m_far &= topo.mask(c, cores[j])
+        m_near = topo.mask(c, cores[near[0]]) & ~m_far
+        return near, far, m_near, m_far
+
+    near, far, m_near, m_far = plan(rank)
+    order = [rank] + near + far
+    levels = [order[FIRST[i]:FIRST[i] + SIZES[i]] for i in range(NL)]
+    last = NL - 1
+
+    def landed(j):
+        nj, fj, mn, mf = plan(j)
+        return _bits(mn) if rank in nj else _bits(mf)
+
+    def slot(j):
+        return T.kv[:, j * 256:(j + 1) * 256]
+
+    def kk(j):
+        return T.kv[:, j * 256:j * 256 + 128]
+
+    def vv(j):
+        return T.kv[:, j * 256 + 128:j * 256 + 256]
+
+    def stb(lv, b):
+        return T["st%d%d" % (lv % 2, b)]
+
+    def col(t, lv, b):
+        return t[:, lv * QB + b:lv * QB + b + 1]
+
+    def blk(t, lv, b):
+        return t[:, (lv * QB + b) * 128:(lv * QB + b + 1) * 128]
+
+    def off(lv, b):
+        return (b * N + FIRST[lv]) * 128
+
+    tp = [T.tp0, T.tp1]
+    yp = [T.yp0, T.yp1]
+
+    sy.dma_start(kk(rank), T.k[:]).then_inc(T.sem.ldk, 16)
+    ac.dma_start(vv(rank), T.v[:]).then_inc(T.sem.ldv, 16)
+    sy.dma_start(T.qs[:], T.q[:]).then_inc(T.sem.ldq, 16)
+
+    ve.memset(T.ident[:], 1.0).then_inc(T.sem.ones, 1)
+    g.wait_ge(T.sem.ones, 1)
+    g.affine_select(T.ident[:], T.ident[:], [[-1, 128]], AluOpType.is_equal, 0.0, 0, 1).then_inc(T.sem.idn, 1)
+    g.wait_ge(T.sem.ldk, 16)
+    g.wait_ge(T.sem.ldv, 16)
+
+    def dst_id(j):
+        rid, pid = topo.addr(cores[j], core)
+        return DstId(rid=rid, pnc=pid)
+
+    arr_me = T.sem["arr%d" % rank]
+    g.remote_dma_fused([
+        RemoteDMATransfer(dst_ids=[dst_id(j) for j in far], dma_engine_mask=m_far, remote_sem=arr_me,
+                          srcs=[slot(rank)], dsts=[slot(rank) for j in far], alu_op=0),
+        RemoteDMATransfer(dst_ids=[dst_id(j) for j in near], dma_engine_mask=m_near, remote_sem=arr_me,
+                          srcs=[slot(rank)], dsts=[slot(rank) for j in near], alu_op=0),
+    ], local_sem=T.sem.sent)
+    g.wait_ge(T.sem.sent, _bits(m_far) + _bits(m_near))
+
+    te.wait_ge(T.sem.ldq, 16)
+    for lv, srcs in enumerate(levels):
+        n = len(srcs)
+        for i, j in enumerate(srcs):
+            if j == rank:
+                te.wait_ge(T.sem.ldk, 16)
+            else:
+                te.wait_ge(T.sem["arr%d" % j], landed(j))
+            for b in range(QB):
+                if lv > 0 and i == 0:
+                    te.wait_ge(S("put", lv, b), 1)
+                te.matmul(stb(lv, b)[:, i * 128:(i + 1) * 128], T.qs[:, b * 128:(b + 1) * 128], kk(j),
+                          start=True, stop=True).then_inc(S("st", lv, b), 1)
+        if lv == 0:
+            te.wait_ge(T.sem.idn, 1)
+        for b in range(QB):
+            te.wait_ge(S("ex", lv, b), 1)
+            for i in range(n):
+                o = off(lv, b) + i * 128
+                te.transpose(tp[b][:, i * 128:(i + 1) * 128], T.p[:, o:o + 128], T.ident[:]).then_inc(S("tr", lv, b), 1)
+        if lv == 0:
+            te.wait_ge(T.sem.ldv, 16)
+        for b in range(QB):
+            te.wait_ge(S("cp", lv, b), 1)
+            if lv > 0:
+                te.wait_ge(S("oc", lv - 1, b), 1)
+            for i, j in enumerate(srcs):
+                o = off(lv, b) + i * 128
+                te.matmul(yp[b][:, 0:128], T.pt[:, o:o + 128], vv(j),
+                          start=(i == 0), stop=(lv == 0 and i == n - 1)).then_inc(S("pv", lv, b), 1)
+            if lv > 0:
+                te.wait_ge(S("df", lv, b), 1)
+                te.matmul(yp[b][:, 0:128], blk(T.df, lv, b), blk(T.op, lv - 1, b),
+                          start=False, stop=True).then_inc(S("pv", lv, b), 1)
+
+    def n_pv(lv):
+        return SIZES[lv] + (1 if lv > 0 else 0)
+
+    for lv in range(NL):
+        n = SIZES[lv]
+        w = n * 128
+        for b in range(QB):
+            ve.wait_ge(S("st", lv, b), n)
+            if lv > 0:
+                ve.wait_ge(S("put", lv, b), 1)
+            ve.tensor_reduce(col(T.negm, lv, b), stb(lv, b)[:, 0:w + (1 if lv > 0 else 0)], AxisListType.X, amax,
+                             negate=True).then_inc(S("red", lv, b), 1)
+        if lv < last:
+            wn = SIZES[lv + 1] * 128
+            for b in range(QB):
+                ve.wait_ge(S("red", lv, b), 1)
+                if lv >= 1:
+                    ve.wait_ge(S("ex", lv - 1, b), 1)
+                ve.tensor_scalar(stb(lv + 1, b)[:, wn:wn + 1], col(T.negm, lv, b), -1.0, None,
+                                 mult).then_inc(S("put", lv + 1, b), 1)
+        for b in range(QB):
+            ve.wait_ge(S("tr", lv, b), n)
+            ve.tensor_copy(T.pt[:, off(lv, b):off(lv, b) + w], tp[b][:, 0:w]).then_inc(S("cp", lv, b), 1)
+            if lv > 0:
+                if lv == 1 and b == 0:
+                    ve.wait_ge(T.sem.idn, 1)
+                ve.wait_ge(S("f", lv, b), 1)
+                ve.tensor_scalar(blk(T.df, lv, b), T.ident[:], col(T.fcol, lv, b), None,
+                                 mult).then_inc(S("df", lv, b), 1)
+                ve.wait_ge(S("ex", lv, b), 1)
+                if lv == 1:
+                    ve.wait_ge(S("ex", 0, b), 1)
+                    before = col(T.lsum, 0, b)
+                else:
+                    ve.wait_ge(S("l", lv - 1, b), 1)
+                    before = col(T.lrun, lv - 1, b)
+                ve.tensor_scalar(col(T.lrun, lv, b), before, col(T.fcol, lv, b), col(T.lsum, lv, b),
+                                 mult, add).then_inc(S("l", lv, b), 1)
+    for b in range(QB):
+        ve.wait_ge(S("l", last, b), 1)
+    ve.reciprocal(T.rinv[:, 0:QB], T.lrun[:, last * QB:(last + 1) * QB]).then_inc(T.sem.rc, 1)
+    ve.wait_ge(T.sem.rc, 1)
+    for b in range(QB):
+        ve.wait_ge(S("pv", last, b), n_pv(last))
+        ve.tensor_scalar(T.ys[:, b * 128:(b + 1) * 128], yp[b][:, 0:128], T.rinv[:, b:b + 1], None,
+                         mult).then_inc(T.sem["ny%d" % b], 1)
+
+    for lv in range(NL):
+        w = SIZES[lv] * 128
+        for b in range(QB):
+            ac.wait_ge(S("red", lv, b), 1)
+            ac.activation(T.p[:, off(lv, b):off(lv, b) + w], stb(lv, b)[:, 0:w], Exp, bias=col(T.negm, lv, b), scale=1.0,
+                          accum_out=col(T.lsum, lv, b)).then_inc(S("ex", lv, b), 1)
+        if lv > 0:
+            for b in range(QB):
+                ac.activation(col(T.fcol, lv, b), col(T.negm, lv - 1, b), Exp, bias=col(T.negm, lv, b),
+                              scale=-1.0).then_inc(S("f", lv, b), 1)
+        if lv < last:
+            for b in range(QB):
+                ac.wait_ge(S("pv", lv, b), n_pv(lv))
+                ac.activation(blk(T.op, lv, b), yp[b][:, 0:128], Copy).then_inc(S("oc", lv, b), 1)
+
+    for b in range(QB):
+        sy.wait_ge(T.sem["ny%d" % b], 1)
+        sy.dma_start(T.y[b * 128:(b + 1) * 128, :], T.ys[:, b * 128:(b + 1) * 128]).then_inc(T.sem.out, 16)
+    sy.wait_ge(T.sem.out, 16 * QB)

@@ -3,9 +3,11 @@ from concourse.mybir import AluOpType, AxisListType, ActivationFunctionType
 
 N = 4
 QB = 2
-SIZES = (1, 1, 2)
-NL = len(SIZES)
-FIRST = tuple(sum(SIZES[:i]) for i in range(NL))
+SIZES = (1, 3)
+FIRST = (0, 1)
+NT = 3
+EXC = {(0, 0): ((0, 1),), (0, 1): ((0, 1),), (1, 0): ((0, 1), (1, 2), (2, 3)), (1, 1): ((0, 3),)}
+CHUNKS = [(lv, b, c) for lv in range(2) for b in range(QB) for c in range(SIZES[lv])]
 
 SCRATCH = {
     "kv": ("sbuf", [128, N * 256], "bfloat16"),
@@ -13,29 +15,29 @@ SCRATCH = {
     "ident": ("sbuf", [128, 128], "bfloat16"),
     "p": ("sbuf", [128, QB * N * 128], "bfloat16"),
     "pt": ("sbuf", [128, QB * N * 128], "bfloat16"),
-    "df": ("sbuf", [128, NL * QB * 128], "bfloat16"),
-    "op": ("sbuf", [128, NL * QB * 128], "bfloat16"),
-    "negm": ("sbuf", [128, NL * QB], "float32"),
-    "lsum": ("sbuf", [128, NL * QB], "float32"),
-    "fcol": ("sbuf", [128, NL * QB], "float32"),
-    "lrun": ("sbuf", [128, NL * QB], "float32"),
+    "df": ("sbuf", [128, QB * 128], "bfloat16"),
+    "op": ("sbuf", [128, QB * 128], "bfloat16"),
+    "negm": ("sbuf", [128, 2 * QB], "float32"),
+    "lsum": ("sbuf", [128, 2 * QB * 3], "float32"),
+    "ssum": ("sbuf", [128, QB], "float32"),
+    "fcol": ("sbuf", [128, QB], "float32"),
+    "lrun": ("sbuf", [128, QB], "float32"),
     "rinv": ("sbuf", [128, QB], "float32"),
     "ys": ("sbuf", [128, QB * 128], "bfloat16"),
-    "st00": ("psum", [128, 512], "float32"), "st01": ("psum", [128, 512], "float32"),
-    "st10": ("psum", [128, 512], "float32"), "st11": ("psum", [128, 512], "float32"),
+    "st0": ("psum", [128, 512], "float32"), "st1": ("psum", [128, 512], "float32"),
     "tp0": ("psum", [128, 1024], "bfloat16"), "tp1": ("psum", [128, 1024], "bfloat16"),
+    "tp2": ("psum", [128, 1024], "bfloat16"),
     "yp0": ("psum", [128, 512], "float32"), "yp1": ("psum", [128, 512], "float32"),
 }
 
-SEMAPHORES = ["ones", "idn", "ldk", "ldv", "ldq", "sent", "rc", "out", "ny0", "ny1"] + ["arr%d" % j for j in range(N)]
-for _g in range(NL):
-    for _b in range(QB):
-        _names = ["st", "red", "ex", "tr", "cp", "pv"]
-        if _g > 0:
-            _names += ["put", "f", "df", "l"]
-        if _g < NL - 1:
-            _names += ["oc"]
-        SEMAPHORES += ["%s%d%d" % (_n, _g, _b) for _n in _names]
+SEMAPHORES = ["ones", "idn", "ldk", "ldv", "ldq", "sent", "rc", "out"] + ["arr%d" % j for j in range(N)]
+for _b in range(QB):
+    SEMAPHORES += ["%s%d" % (_n, _b) for _n in ("ny", "put", "f", "df", "l", "oc", "ss")]
+    for _lv in range(2):
+        SEMAPHORES += ["%s%d%d" % (_n, _lv, _b) for _n in ("st", "red", "pv")]
+        SEMAPHORES += ["ex%d%d%d" % (_lv, _b, _e) for _e in range(len(EXC[_lv, _b]))]
+        SEMAPHORES += ["%s%d%d%d" % (_n, _lv, _b, _c) for _n in ("tr", "cp") for _c in range(SIZES[_lv])]
+SEMAPHORES.remove("ss1")
 
 
 def _bits(m):
@@ -51,8 +53,8 @@ def rank_program(g, core, T, topo):
     Exp, Copy = ActivationFunctionType.Exp, ActivationFunctionType.Copy
     mult, add, amax = AluOpType.mult, AluOpType.add, AluOpType.max
 
-    def S(name, lv, b):
-        return T.sem["%s%d%d" % (name, lv, b)]
+    def S(name, *idx):
+        return T.sem[name + "".join("%d" % i for i in idx)]
 
     def plan(r):
         c = cores[r]
@@ -68,8 +70,7 @@ def rank_program(g, core, T, topo):
 
     near, far, m_near, m_far = plan(rank)
     order = [rank] + near + far
-    levels = [order[FIRST[i]:FIRST[i] + SIZES[i]] for i in range(NL)]
-    last = NL - 1
+    levels = [order[FIRST[i]:FIRST[i] + SIZES[i]] for i in range(2)]
 
     def landed(j):
         nj, fj, mn, mf = plan(j)
@@ -84,20 +85,22 @@ def rank_program(g, core, T, topo):
     def vv(j):
         return T.kv[:, j * 256 + 128:j * 256 + 256]
 
-    def stb(lv, b):
-        return T["st%d%d" % (lv % 2, b)]
+    def col(t, i):
+        return t[:, i:i + 1]
 
-    def col(t, lv, b):
-        return t[:, lv * QB + b:lv * QB + b + 1]
+    def blk(t, b):
+        return t[:, b * 128:(b + 1) * 128]
 
-    def blk(t, lv, b):
-        return t[:, (lv * QB + b) * 128:(lv * QB + b + 1) * 128]
+    def off(lv, b, c):
+        return (b * N + FIRST[lv] + c) * 128
 
-    def off(lv, b):
-        return (b * N + FIRST[lv]) * 128
+    def lcol(lv, b, e):
+        return (lv * QB + b) * 3 + e
 
-    tp = [T.tp0, T.tp1]
+    st = [T.st0, T.st1]
+    tp = [T.tp0, T.tp1, T.tp2]
     yp = [T.yp0, T.yp1]
+    W1 = SIZES[1] * 128
 
     sy.dma_start(kk(rank), T.k[:]).then_inc(T.sem.ldk, 16)
     ac.dma_start(vv(rank), T.v[:]).then_inc(T.sem.ldv, 16)
@@ -122,104 +125,128 @@ def rank_program(g, core, T, topo):
     ], local_sem=T.sem.sent)
     g.wait_ge(T.sem.sent, _bits(m_far) + _bits(m_near))
 
-    te.wait_ge(T.sem.ldq, 16)
-    for lv, srcs in enumerate(levels):
-        n = len(srcs)
-        for i, j in enumerate(srcs):
-            if j == rank:
-                te.wait_ge(T.sem.ldk, 16)
+    def scores(lv, b, c):
+        te.matmul(st[b][:, c * 128:(c + 1) * 128], blk(T.qs, b), kk(levels[lv][c]),
+                  start=True, stop=True).then_inc(S("st", lv, b), 1)
+
+    def transposes(lv, b):
+        for e, (c0, c1) in enumerate(EXC[lv, b]):
+            te.wait_ge(S("ex", lv, b, e), 1)
+            for c in range(c0, c1):
+                k = CHUNKS.index((lv, b, c))
+                if k >= NT:
+                    te.wait_ge(S("cp", *CHUNKS[k - NT]), 1)
+                o = off(lv, b, c)
+                te.transpose(tp[k % NT][:, 0:128], T.p[:, o:o + 128], T.ident[:]).then_inc(S("tr", lv, b, c), 1)
+
+    def weighted(lv, b):
+        ops = list(range(SIZES[lv]))
+        if lv > 0:
+            ops.insert(len(ops) - b, -1)
+            te.wait_ge(S("oc", b), 1)
+        for i, c in enumerate(ops):
+            if c < 0:
+                te.wait_ge(S("df", b), 1)
+                lhsT, rhs = blk(T.df, b), blk(T.op, b)
             else:
-                te.wait_ge(T.sem["arr%d" % j], landed(j))
-            for b in range(QB):
-                if lv > 0 and i == 0:
-                    te.wait_ge(S("put", lv, b), 1)
-                te.matmul(stb(lv, b)[:, i * 128:(i + 1) * 128], T.qs[:, b * 128:(b + 1) * 128], kk(j),
-                          start=True, stop=True).then_inc(S("st", lv, b), 1)
-        if lv == 0:
-            te.wait_ge(T.sem.idn, 1)
-        for b in range(QB):
-            te.wait_ge(S("ex", lv, b), 1)
-            for i in range(n):
-                o = off(lv, b) + i * 128
-                te.transpose(tp[b][:, i * 128:(i + 1) * 128], T.p[:, o:o + 128], T.ident[:]).then_inc(S("tr", lv, b), 1)
-        if lv == 0:
-            te.wait_ge(T.sem.ldv, 16)
-        for b in range(QB):
-            te.wait_ge(S("cp", lv, b), 1)
-            if lv > 0:
-                te.wait_ge(S("oc", lv - 1, b), 1)
-            for i, j in enumerate(srcs):
-                o = off(lv, b) + i * 128
-                te.matmul(yp[b][:, 0:128], T.pt[:, o:o + 128], vv(j),
-                          start=(i == 0), stop=(lv == 0 and i == n - 1)).then_inc(S("pv", lv, b), 1)
-            if lv > 0:
-                te.wait_ge(S("df", lv, b), 1)
-                te.matmul(yp[b][:, 0:128], blk(T.df, lv, b), blk(T.op, lv - 1, b),
-                          start=False, stop=True).then_inc(S("pv", lv, b), 1)
+                te.wait_ge(S("cp", lv, b, c), 1)
+                o = off(lv, b, c)
+                lhsT, rhs = T.pt[:, o:o + 128], vv(levels[lv][c])
+            te.matmul(yp[b][:, 0:128], lhsT, rhs, start=(i == 0), stop=(i == len(ops) - 1)).then_inc(S("pv", lv, b), 1)
 
-    def n_pv(lv):
-        return SIZES[lv] + (1 if lv > 0 else 0)
-
-    for lv in range(NL):
-        n = SIZES[lv]
-        w = n * 128
-        for b in range(QB):
-            ve.wait_ge(S("st", lv, b), n)
-            if lv > 0:
-                ve.wait_ge(S("put", lv, b), 1)
-            ve.tensor_reduce(col(T.negm, lv, b), stb(lv, b)[:, 0:w + (1 if lv > 0 else 0)], AxisListType.X, amax,
-                             negate=True).then_inc(S("red", lv, b), 1)
-        if lv < last:
-            wn = SIZES[lv + 1] * 128
-            for b in range(QB):
-                ve.wait_ge(S("red", lv, b), 1)
-                if lv >= 1:
-                    ve.wait_ge(S("ex", lv - 1, b), 1)
-                ve.tensor_scalar(stb(lv + 1, b)[:, wn:wn + 1], col(T.negm, lv, b), -1.0, None,
-                                 mult).then_inc(S("put", lv + 1, b), 1)
-        for b in range(QB):
-            ve.wait_ge(S("tr", lv, b), n)
-            ve.tensor_copy(T.pt[:, off(lv, b):off(lv, b) + w], tp[b][:, 0:w]).then_inc(S("cp", lv, b), 1)
-            if lv > 0:
-                if lv == 1 and b == 0:
-                    ve.wait_ge(T.sem.idn, 1)
-                ve.wait_ge(S("f", lv, b), 1)
-                ve.tensor_scalar(blk(T.df, lv, b), T.ident[:], col(T.fcol, lv, b), None,
-                                 mult).then_inc(S("df", lv, b), 1)
-                ve.wait_ge(S("ex", lv, b), 1)
-                if lv == 1:
-                    ve.wait_ge(S("ex", 0, b), 1)
-                    before = col(T.lsum, 0, b)
-                else:
-                    ve.wait_ge(S("l", lv - 1, b), 1)
-                    before = col(T.lrun, lv - 1, b)
-                ve.tensor_scalar(col(T.lrun, lv, b), before, col(T.fcol, lv, b), col(T.lsum, lv, b),
-                                 mult, add).then_inc(S("l", lv, b), 1)
+    te.wait_ge(T.sem.ldq, 16)
+    te.wait_ge(T.sem.ldk, 16)
     for b in range(QB):
-        ve.wait_ge(S("l", last, b), 1)
-    ve.reciprocal(T.rinv[:, 0:QB], T.lrun[:, last * QB:(last + 1) * QB]).then_inc(T.sem.rc, 1)
+        scores(0, b, 0)
+    te.wait_ge(T.sem.idn, 1)
+    for b in range(QB):
+        transposes(0, b)
+    te.wait_ge(T.sem.ldv, 16)
+    for b in range(QB):
+        weighted(0, b)
+    for b in range(QB):
+        te.wait_ge(S("put", b), 1)
+    te.wait_ge(T.sem["arr%d" % levels[1][0]], landed(levels[1][0]))
+    for b in range(QB):
+        scores(1, b, 0)
+    for c in (1, 2):
+        te.wait_ge(T.sem["arr%d" % levels[1][c]], landed(levels[1][c]))
+        scores(1, 0, c)
+    for c in (1, 2):
+        scores(1, 1, c)
+    for b in range(QB):
+        transposes(1, b)
+        weighted(1, b)
+
+    for b in range(QB):
+        ve.wait_ge(S("st", 0, b), 1)
+        ve.tensor_reduce(col(T.negm, b), st[b][:, 0:128], AxisListType.X, amax, negate=True).then_inc(S("red", 0, b), 1)
+    for b in range(QB):
+        ve.wait_ge(S("tr", 0, b, 0), 1)
+        k = CHUNKS.index((0, b, 0))
+        o = off(0, b, 0)
+        ve.tensor_copy(T.pt[:, o:o + 128], tp[k % NT][:, 0:128]).then_inc(S("cp", 0, b, 0), 1)
+    for b in range(QB):
+        ve.wait_ge(S("red", 0, b), 1)
+        ve.wait_ge(S("ex", 0, b, 0), 1)
+        ve.tensor_scalar(st[b][:, W1:W1 + 1], col(T.negm, b), -1.0, None, mult).then_inc(S("put", b), 1)
+    for b in range(QB):
+        ve.wait_ge(S("st", 1, b), SIZES[1])
+        ve.wait_ge(S("put", b), 1)
+        ve.tensor_reduce(col(T.negm, QB + b), st[b][:, 0:W1 + 1], AxisListType.X, amax,
+                         negate=True).then_inc(S("red", 1, b), 1)
+    for c in range(SIZES[1]):
+        ve.wait_ge(S("tr", 1, 0, c), 1)
+        k = CHUNKS.index((1, 0, c))
+        o = off(1, 0, c)
+        ve.tensor_copy(T.pt[:, o:o + 128], tp[k % NT][:, 0:128]).then_inc(S("cp", 1, 0, c), 1)
+    ve.wait_ge(T.sem.idn, 1)
+    for b in range(QB):
+        ve.wait_ge(S("f", b), 1)
+        ve.tensor_scalar(blk(T.df, b), T.ident[:], col(T.fcol, b), None, mult).then_inc(S("df", b), 1)
+        ne = len(EXC[1, b])
+        for e in range(ne):
+            ve.wait_ge(S("ex", 1, b, e), 1)
+        if ne > 1:
+            ve.tensor_reduce(col(T.ssum, b), T.lsum[:, lcol(1, b, 0):lcol(1, b, 0) + ne], AxisListType.X,
+                             add).then_inc(S("ss", b), 1)
+            ve.wait_ge(S("ss", b), 1)
+            sums = col(T.ssum, b)
+        else:
+            sums = col(T.lsum, lcol(1, b, 0))
+        ve.tensor_scalar(col(T.lrun, b), col(T.lsum, lcol(0, b, 0)), col(T.fcol, b), sums,
+                         mult, add).then_inc(S("l", b), 1)
+    for b in range(QB):
+        ve.wait_ge(S("l", b), 1)
+    ve.reciprocal(T.rinv[:, 0:QB], T.lrun[:, 0:QB]).then_inc(T.sem.rc, 1)
     ve.wait_ge(T.sem.rc, 1)
     for b in range(QB):
-        ve.wait_ge(S("pv", last, b), n_pv(last))
-        ve.tensor_scalar(T.ys[:, b * 128:(b + 1) * 128], yp[b][:, 0:128], T.rinv[:, b:b + 1], None,
-                         mult).then_inc(T.sem["ny%d" % b], 1)
+        ve.wait_ge(S("pv", 1, b), SIZES[1] + 1)
+        ve.tensor_scalar(blk(T.ys, b), yp[b][:, 0:128], col(T.rinv, b), None, mult).then_inc(S("ny", b), 1)
 
-    for lv in range(NL):
-        w = SIZES[lv] * 128
-        for b in range(QB):
-            ac.wait_ge(S("red", lv, b), 1)
-            ac.activation(T.p[:, off(lv, b):off(lv, b) + w], stb(lv, b)[:, 0:w], Exp, bias=col(T.negm, lv, b), scale=1.0,
-                          accum_out=col(T.lsum, lv, b)).then_inc(S("ex", lv, b), 1)
-        if lv > 0:
-            for b in range(QB):
-                ac.activation(col(T.fcol, lv, b), col(T.negm, lv - 1, b), Exp, bias=col(T.negm, lv, b),
-                              scale=-1.0).then_inc(S("f", lv, b), 1)
-        if lv < last:
-            for b in range(QB):
-                ac.wait_ge(S("pv", lv, b), n_pv(lv))
-                ac.activation(blk(T.op, lv, b), yp[b][:, 0:128], Copy).then_inc(S("oc", lv, b), 1)
+    def exps(lv, b):
+        ac.wait_ge(S("red", lv, b), 1)
+        for e, (c0, c1) in enumerate(EXC[lv, b]):
+            ac.activation(T.p[:, off(lv, b, c0):off(lv, b, c1)], st[b][:, c0 * 128:c1 * 128], Exp,
+                          bias=col(T.negm, lv * QB + b), scale=1.0,
+                          accum_out=col(T.lsum, lcol(lv, b, e))).then_inc(S("ex", lv, b, e), 1)
 
     for b in range(QB):
-        sy.wait_ge(T.sem["ny%d" % b], 1)
-        sy.dma_start(T.y[b * 128:(b + 1) * 128, :], T.ys[:, b * 128:(b + 1) * 128]).then_inc(T.sem.out, 16)
+        exps(0, b)
+    for b in range(QB):
+        ac.wait_ge(S("pv", 0, b), 1)
+        ac.activation(blk(T.op, b), yp[b][:, 0:128], Copy).then_inc(S("oc", b), 1)
+    for b in range(QB):
+        exps(1, b)
+        ac.activation(col(T.fcol, b), col(T.negm, b), Exp, bias=col(T.negm, QB + b),
+                      scale=-1.0).then_inc(S("f", b), 1)
+    for c in range(SIZES[1]):
+        ac.wait_ge(S("tr", 1, 1, c), 1)
+        k = CHUNKS.index((1, 1, c))
+        o = off(1, 1, c)
+        ac.activation(T.pt[:, o:o + 128], tp[k % NT][:, 0:128], Copy).then_inc(S("cp", 1, 1, c), 1)
+
+    for b in range(QB):
+        sy.wait_ge(S("ny", b), 1)
+        sy.dma_start(T.y[b * 128:(b + 1) * 128, :], blk(T.ys, b)).then_inc(T.sem.out, 16)
     sy.wait_ge(T.sem.out, 16 * QB)

@@ -28,13 +28,15 @@ SCRATCH = {
     "tp0": ("psum", [128, 1024], "bfloat16"), "tp1": ("psum", [128, 1024], "bfloat16"),
     "tp2": ("psum", [128, 1024], "bfloat16"),
     "yp0": ("psum", [128, 512], "float32"), "yp1": ("psum", [128, 512], "float32"),
+    "yo": ("psum", [128, 512], "float32"),
 }
 
-SEMAPHORES = ["ones", "idn", "ldk", "ldv", "ldq", "sent", "rc", "out"] + ["arr%d" % j for j in range(N)]
+SEMAPHORES = ["ones", "idn", "ldk", "ldv", "ldq", "sent", "rc", "out", "pvo", "oc"]
+SEMAPHORES += ["ak%d" % j for j in range(N)] + ["av%d" % j for j in range(N)]
 for _b in range(QB):
-    SEMAPHORES += ["%s%d" % (_n, _b) for _n in ("ny", "put", "f", "df", "l", "oc", "ss")]
+    SEMAPHORES += ["%s%d" % (_n, _b) for _n in ("ny", "put", "f", "df", "l", "ss", "pv")]
     for _lv in range(2):
-        SEMAPHORES += ["%s%d%d" % (_n, _lv, _b) for _n in ("st", "red", "pv")]
+        SEMAPHORES += ["%s%d%d" % (_n, _lv, _b) for _n in ("st", "red")]
         SEMAPHORES += ["ex%d%d%d" % (_lv, _b, _e) for _e in range(len(EXC[_lv, _b]))]
         SEMAPHORES += ["%s%d%d%d" % (_n, _lv, _b, _c) for _n in ("tr", "cp") for _c in range(SIZES[_lv])]
 SEMAPHORES.remove("ss1")
@@ -76,9 +78,6 @@ def rank_program(g, core, T, topo):
         nj, fj, mn, mf = plan(j)
         return _bits(mn) if rank in nj else _bits(mf)
 
-    def slot(j):
-        return T.kv[:, j * 256:(j + 1) * 256]
-
     def kk(j):
         return T.kv[:, j * 256:j * 256 + 128]
 
@@ -97,36 +96,39 @@ def rank_program(g, core, T, topo):
     def lcol(lv, b, e):
         return (lv * QB + b) * 3 + e
 
-    st = [T.st0, T.st1]
     tp = [T.tp0, T.tp1, T.tp2]
     yp = [T.yp0, T.yp1]
+    st = [yp, [T.st0, T.st1]]
     W1 = SIZES[1] * 128
 
     sy.dma_start(kk(rank), T.k[:]).then_inc(T.sem.ldk, 16)
-    ac.dma_start(vv(rank), T.v[:]).then_inc(T.sem.ldv, 16)
-    sy.dma_start(T.qs[:], T.q[:]).then_inc(T.sem.ldq, 16)
+    ac.dma_start(T.qs[:], T.q[:]).then_inc(T.sem.ldq, 16)
+    sy.dma_start(vv(rank), T.v[:]).then_inc(T.sem.ldv, 16)
 
     ve.memset(T.ident[:], 1.0).then_inc(T.sem.ones, 1)
     g.wait_ge(T.sem.ones, 1)
     g.affine_select(T.ident[:], T.ident[:], [[-1, 128]], AluOpType.is_equal, 0.0, 0, 1).then_inc(T.sem.idn, 1)
-    g.wait_ge(T.sem.ldk, 16)
-    g.wait_ge(T.sem.ldv, 16)
 
     def dst_id(j):
         rid, pid = topo.addr(cores[j], core)
         return DstId(rid=rid, pnc=pid)
 
-    arr_me = T.sem["arr%d" % rank]
-    g.remote_dma_fused([
-        RemoteDMATransfer(dst_ids=[dst_id(j) for j in far], dma_engine_mask=m_far, remote_sem=arr_me,
-                          srcs=[slot(rank)], dsts=[slot(rank) for j in far], alu_op=0),
-        RemoteDMATransfer(dst_ids=[dst_id(j) for j in near], dma_engine_mask=m_near, remote_sem=arr_me,
-                          srcs=[slot(rank)], dsts=[slot(rank) for j in near], alu_op=0),
-    ], local_sem=T.sem.sent)
-    g.wait_ge(T.sem.sent, _bits(m_far) + _bits(m_near))
+    def send(piece, sem_there):
+        g.remote_dma_fused([
+            RemoteDMATransfer(dst_ids=[dst_id(j) for j in far], dma_engine_mask=m_far, remote_sem=sem_there,
+                              srcs=[piece], dsts=[piece for j in far], alu_op=0),
+            RemoteDMATransfer(dst_ids=[dst_id(j) for j in near], dma_engine_mask=m_near, remote_sem=sem_there,
+                              srcs=[piece], dsts=[piece for j in near], alu_op=0),
+        ], local_sem=T.sem.sent)
+
+    g.wait_ge(T.sem.ldk, 16)
+    send(kk(rank), S("ak", rank))
+    g.wait_ge(T.sem.ldv, 16)
+    send(vv(rank), S("av", rank))
+    g.wait_ge(T.sem.sent, 2 * (_bits(m_far) + _bits(m_near)))
 
     def scores(lv, b, c):
-        te.matmul(st[b][:, c * 128:(c + 1) * 128], blk(T.qs, b), kk(levels[lv][c]),
+        te.matmul(st[lv][b][:, c * 128:(c + 1) * 128], blk(T.qs, b), kk(levels[lv][c]),
                   start=True, stop=True).then_inc(S("st", lv, b), 1)
 
     def transposes(lv, b):
@@ -139,20 +141,16 @@ def rank_program(g, core, T, topo):
                 o = off(lv, b, c)
                 te.transpose(tp[k % NT][:, 0:128], T.p[:, o:o + 128], T.ident[:]).then_inc(S("tr", lv, b, c), 1)
 
-    def weighted(lv, b):
-        ops = list(range(SIZES[lv]))
-        if lv > 0:
-            ops.insert(len(ops) - b, -1)
-            te.wait_ge(S("oc", b), 1)
-        for i, c in enumerate(ops):
-            if c < 0:
-                te.wait_ge(S("df", b), 1)
-                lhsT, rhs = blk(T.df, b), blk(T.op, b)
-            else:
-                te.wait_ge(S("cp", lv, b, c), 1)
-                o = off(lv, b, c)
-                lhsT, rhs = T.pt[:, o:o + 128], vv(levels[lv][c])
-            te.matmul(yp[b][:, 0:128], lhsT, rhs, start=(i == 0), stop=(i == len(ops) - 1)).then_inc(S("pv", lv, b), 1)
+    def weighted(b, c, start, stop):
+        te.wait_ge(S("cp", 1, b, c), 1)
+        if b == 0:
+            te.wait_ge(S("av", levels[1][c]), landed(levels[1][c]))
+        o = off(1, b, c)
+        te.matmul(yp[b][:, 0:128], T.pt[:, o:o + 128], vv(levels[1][c]), start=start, stop=stop).then_inc(S("pv", b), 1)
+
+    def own_share(b, stop):
+        te.wait_ge(S("df", b), 1)
+        te.matmul(yp[b][:, 0:128], blk(T.df, b), blk(T.op, b), start=False, stop=stop).then_inc(S("pv", b), 1)
 
     te.wait_ge(T.sem.ldq, 16)
     te.wait_ge(T.sem.ldk, 16)
@@ -161,39 +159,45 @@ def rank_program(g, core, T, topo):
     te.wait_ge(T.sem.idn, 1)
     for b in range(QB):
         transposes(0, b)
-    te.wait_ge(T.sem.ldv, 16)
-    for b in range(QB):
-        weighted(0, b)
     for b in range(QB):
         te.wait_ge(S("put", b), 1)
-    te.wait_ge(T.sem["arr%d" % levels[1][0]], landed(levels[1][0]))
     for b in range(QB):
-        scores(1, b, 0)
-    for c in (1, 2):
-        te.wait_ge(T.sem["arr%d" % levels[1][c]], landed(levels[1][c]))
-        scores(1, 0, c)
-    for c in (1, 2):
-        scores(1, 1, c)
+        for c in range(SIZES[1]):
+            if b == 0:
+                te.wait_ge(S("ak", levels[1][c]), landed(levels[1][c]))
+            scores(1, b, c)
+    te.wait_ge(T.sem.ldv, 16)
     for b in range(QB):
-        transposes(1, b)
-        weighted(1, b)
+        te.wait_ge(S("cp", 0, b, 0), 1)
+        o = off(0, b, 0)
+        te.matmul(blk(T.yo, b), T.pt[:, o:o + 128], vv(rank), start=True, stop=True).then_inc(T.sem.pvo, 1)
+    transposes(1, 0)
+    for c in range(3):
+        weighted(0, c, c == 0, False)
+    transposes(1, 1)
+    te.wait_ge(T.sem.oc, 1)
+    own_share(0, True)
+    weighted(1, 0, True, False)
+    weighted(1, 1, False, False)
+    own_share(1, False)
+    weighted(1, 2, False, True)
 
     for b in range(QB):
         ve.wait_ge(S("st", 0, b), 1)
-        ve.tensor_reduce(col(T.negm, b), st[b][:, 0:128], AxisListType.X, amax, negate=True).then_inc(S("red", 0, b), 1)
+        ve.tensor_reduce(col(T.negm, b), st[0][b][:, 0:128], AxisListType.X, amax,
+                         negate=True).then_inc(S("red", 0, b), 1)
+    for b in range(QB):
+        ve.wait_ge(S("red", 0, b), 1)
+        ve.tensor_scalar(st[1][b][:, W1:W1 + 1], col(T.negm, b), -1.0, None, mult).then_inc(S("put", b), 1)
     for b in range(QB):
         ve.wait_ge(S("tr", 0, b, 0), 1)
         k = CHUNKS.index((0, b, 0))
         o = off(0, b, 0)
         ve.tensor_copy(T.pt[:, o:o + 128], tp[k % NT][:, 0:128]).then_inc(S("cp", 0, b, 0), 1)
     for b in range(QB):
-        ve.wait_ge(S("red", 0, b), 1)
-        ve.wait_ge(S("ex", 0, b, 0), 1)
-        ve.tensor_scalar(st[b][:, W1:W1 + 1], col(T.negm, b), -1.0, None, mult).then_inc(S("put", b), 1)
-    for b in range(QB):
         ve.wait_ge(S("st", 1, b), SIZES[1])
         ve.wait_ge(S("put", b), 1)
-        ve.tensor_reduce(col(T.negm, QB + b), st[b][:, 0:W1 + 1], AxisListType.X, amax,
+        ve.tensor_reduce(col(T.negm, QB + b), st[1][b][:, 0:W1 + 1], AxisListType.X, amax,
                          negate=True).then_inc(S("red", 1, b), 1)
     for c in range(SIZES[1]):
         ve.wait_ge(S("tr", 1, 0, c), 1)
@@ -214,6 +218,7 @@ def rank_program(g, core, T, topo):
             sums = col(T.ssum, b)
         else:
             sums = col(T.lsum, lcol(1, b, 0))
+        ve.wait_ge(S("ex", 0, b, 0), 1)
         ve.tensor_scalar(col(T.lrun, b), col(T.lsum, lcol(0, b, 0)), col(T.fcol, b), sums,
                          mult, add).then_inc(S("l", b), 1)
     for b in range(QB):
@@ -221,25 +226,24 @@ def rank_program(g, core, T, topo):
     ve.reciprocal(T.rinv[:, 0:QB], T.lrun[:, 0:QB]).then_inc(T.sem.rc, 1)
     ve.wait_ge(T.sem.rc, 1)
     for b in range(QB):
-        ve.wait_ge(S("pv", 1, b), SIZES[1] + 1)
+        ve.wait_ge(S("pv", b), SIZES[1] + 1)
         ve.tensor_scalar(blk(T.ys, b), yp[b][:, 0:128], col(T.rinv, b), None, mult).then_inc(S("ny", b), 1)
 
     def exps(lv, b):
         ac.wait_ge(S("red", lv, b), 1)
         for e, (c0, c1) in enumerate(EXC[lv, b]):
-            ac.activation(T.p[:, off(lv, b, c0):off(lv, b, c1)], st[b][:, c0 * 128:c1 * 128], Exp,
+            ac.activation(T.p[:, off(lv, b, c0):off(lv, b, c1)], st[lv][b][:, c0 * 128:c1 * 128], Exp,
                           bias=col(T.negm, lv * QB + b), scale=1.0,
                           accum_out=col(T.lsum, lcol(lv, b, e))).then_inc(S("ex", lv, b, e), 1)
 
     for b in range(QB):
         exps(0, b)
     for b in range(QB):
-        ac.wait_ge(S("pv", 0, b), 1)
-        ac.activation(blk(T.op, b), yp[b][:, 0:128], Copy).then_inc(S("oc", b), 1)
-    for b in range(QB):
         exps(1, b)
         ac.activation(col(T.fcol, b), col(T.negm, b), Exp, bias=col(T.negm, QB + b),
                       scale=-1.0).then_inc(S("f", b), 1)
+    ac.wait_ge(T.sem.pvo, QB)
+    ac.activation(T.op[:, 0:QB * 128], T.yo[:, 0:QB * 128], Copy).then_inc(T.sem.oc, 1)
     for c in range(SIZES[1]):
         ac.wait_ge(S("tr", 1, 1, c), 1)
         k = CHUNKS.index((1, 1, c))

from concourse.bass import DstId, RemoteDMATransfer
from concourse.mybir import AluOpType, AxisListType, ActivationFunctionType

N = 4
QB = 2
SIZES = (1, 3)
FIRST = (0, 1)
NT = 3
EXC = {(0, 0): ((0, 1),), (0, 1): ((0, 1),), (1, 0): ((0, 1), (1, 2), (2, 3)), (1, 1): ((0, 3),)}
CHUNKS = [(lv, b, c) for lv in range(2) for b in range(QB) for c in range(SIZES[lv])]

SCRATCH = {
    "kv": ("sbuf", [128, N * 256], "bfloat16"),
    "qs": ("sbuf", [128, QB * 128], "bfloat16"),
    "ident": ("sbuf", [128, 128], "bfloat16"),
    "p": ("sbuf", [128, QB * N * 128], "bfloat16"),
    "pt": ("sbuf", [128, QB * N * 128], "bfloat16"),
    "df": ("sbuf", [128, QB * 128], "bfloat16"),
    "op": ("sbuf", [128, QB * 128], "bfloat16"),
    "negm": ("sbuf", [128, 2 * QB], "float32"),
    "lsum": ("sbuf", [128, 2 * QB * 3], "float32"),
    "ssum": ("sbuf", [128, QB], "float32"),
    "fcol": ("sbuf", [128, QB], "float32"),
    "lrun": ("sbuf", [128, QB], "float32"),
    "rinv": ("sbuf", [128, QB], "float32"),
    "ys": ("sbuf", [128, QB * 128], "bfloat16"),
    "st0": ("psum", [128, 512], "float32"), "st1": ("psum", [128, 512], "float32"),
    "tp0": ("psum", [128, 1024], "bfloat16"), "tp1": ("psum", [128, 1024], "bfloat16"),
    "tp2": ("psum", [128, 1024], "bfloat16"),
    "yp0": ("psum", [128, 512], "float32"), "yp1": ("psum", [128, 512], "float32"),
    "yo": ("psum", [128, 512], "float32"),
}

SEMAPHORES = ["ones", "idn", "ldk", "ldv", "ldq", "sent", "rc", "out", "pvo", "oc"]
SEMAPHORES += ["ak%d" % j for j in range(N)] + ["av%d" % j for j in range(N)]
for _b in range(QB):
    SEMAPHORES += ["%s%d" % (_n, _b) for _n in ("ny", "put", "f", "df", "l", "ss", "pv")]
    for _lv in range(2):
        SEMAPHORES += ["%s%d%d" % (_n, _lv, _b) for _n in ("st", "red")]
        SEMAPHORES += ["ex%d%d%d" % (_lv, _b, _e) for _e in range(len(EXC[_lv, _b]))]
        SEMAPHORES += ["%s%d%d%d" % (_n, _lv, _b, _c) for _n in ("tr", "cp") for _c in range(SIZES[_lv])]
SEMAPHORES.remove("ss1")


def _bits(m):
    return bin(m).count("1")


def rank_program(g, core, T, topo):
    rank = T.rank_of(core)
    if rank is None:
        return
    cores = T.cores
    te, ve, ac, sy = g.tensor, g.vector, g.scalar, g.sync
    Exp, Copy = ActivationFunctionType.Exp, ActivationFunctionType.Copy
    mult, add, amax = AluOpType.mult, AluOpType.add, AluOpType.max

    def S(name, *idx):
        return T.sem[name + "".join("%d" % i for i in idx)]

    def plan(r):
        c = cores[r]
        here = lambda j: topo.host(cores[j]) == topo.host(c) and topo.chip(cores[j]) == topo.chip(c)
        near = [j for j in range(N) if j != r and here(j)]
        far = [j for j in range(N) if j != r and not here(j)]
        far.sort(key=lambda j: topo.die(cores[j]) != topo.die(c))
        m_far = topo.mask(c, cores[far[0]])
        for j in far:
            m_far &= topo.mask(c, cores[j])
        m_near = topo.mask(c, cores[near[0]]) & ~m_far
        return near, far, m_near, m_far

    near, far, m_near, m_far = plan(rank)
    order = [rank] + near + far
    levels = [order[FIRST[i]:FIRST[i] + SIZES[i]] for i in range(2)]

    def landed(j):
        nj, fj, mn, mf = plan(j)
        return _bits(mn) if rank in nj else _bits(mf)

    def kk(j):
        return T.kv[:, j * 256:j * 256 + 128]

    def vv(j):
        return T.kv[:, j * 256 + 128:j * 256 + 256]

    def col(t, i):
        return t[:, i:i + 1]

    def blk(t, b):
        return t[:, b * 128:(b + 1) * 128]

    def off(lv, b, c):
        return (b * N + FIRST[lv] + c) * 128

    def lcol(lv, b, e):
        return (lv * QB + b) * 3 + e

    tp = [T.tp0, T.tp1, T.tp2]
    yp = [T.yp0, T.yp1]
    st = [yp, [T.st0, T.st1]]
    W1 = SIZES[1] * 128

    sy.dma_start(kk(rank), T.k[:]).then_inc(T.sem.ldk, 16)
    ac.dma_start(T.qs[:], T.q[:]).then_inc(T.sem.ldq, 16)
    sy.dma_start(vv(rank), T.v[:]).then_inc(T.sem.ldv, 16)

    ve.memset(T.ident[:], 1.0).then_inc(T.sem.ones, 1)
    g.wait_ge(T.sem.ones, 1)
    g.affine_select(T.ident[:], T.ident[:], [[-1, 128]], AluOpType.is_equal, 0.0, 0, 1).then_inc(T.sem.idn, 1)

    def dst_id(j):
        rid, pid = topo.addr(cores[j], core)
        return DstId(rid=rid, pnc=pid)

    def send(piece, sem_there):
        g.remote_dma_fused([
            RemoteDMATransfer(dst_ids=[dst_id(j) for j in far], dma_engine_mask=m_far, remote_sem=sem_there,
                              srcs=[piece], dsts=[piece for j in far], alu_op=0),
            RemoteDMATransfer(dst_ids=[dst_id(j) for j in near], dma_engine_mask=m_near, remote_sem=sem_there,
                              srcs=[piece], dsts=[piece for j in near], alu_op=0),
        ], local_sem=T.sem.sent)

    g.wait_ge(T.sem.ldk, 16)
    send(kk(rank), S("ak", rank))
    g.wait_ge(T.sem.ldv, 16)
    send(vv(rank), S("av", rank))
    g.wait_ge(T.sem.sent, 2 * (_bits(m_far) + _bits(m_near)))

    def scores(lv, b, c):
        te.matmul(st[lv][b][:, c * 128:(c + 1) * 128], blk(T.qs, b), kk(levels[lv][c]),
                  start=True, stop=True).then_inc(S("st", lv, b), 1)

    def transposes(lv, b):
        for e, (c0, c1) in enumerate(EXC[lv, b]):
            te.wait_ge(S("ex", lv, b, e), 1)
            for c in range(c0, c1):
                k = CHUNKS.index((lv, b, c))
                if k >= NT:
                    te.wait_ge(S("cp", *CHUNKS[k - NT]), 1)
                o = off(lv, b, c)
                te.transpose(tp[k % NT][:, 0:128], T.p[:, o:o + 128], T.ident[:]).then_inc(S("tr", lv, b, c), 1)

    def weighted(b, c, start, stop):
        te.wait_ge(S("cp", 1, b, c), 1)
        if b == 0:
            te.wait_ge(S("av", levels[1][c]), landed(levels[1][c]))
        o = off(1, b, c)
        te.matmul(yp[b][:, 0:128], T.pt[:, o:o + 128], vv(levels[1][c]), start=start, stop=stop).then_inc(S("pv", b), 1)

    def own_share(b, stop):
        te.wait_ge(S("df", b), 1)
        te.matmul(yp[b][:, 0:128], blk(T.df, b), blk(T.op, b), start=False, stop=stop).then_inc(S("pv", b), 1)

    te.wait_ge(T.sem.ldq, 16)
    te.wait_ge(T.sem.ldk, 16)
    for b in range(QB):
        scores(0, b, 0)
    te.wait_ge(T.sem.idn, 1)
    for b in range(QB):
        transposes(0, b)
    for b in range(QB):
        te.wait_ge(S("put", b), 1)
    for b in range(QB):
        for c in range(SIZES[1]):
            if b == 0:
                te.wait_ge(S("ak", levels[1][c]), landed(levels[1][c]))
            scores(1, b, c)
    te.wait_ge(T.sem.ldv, 16)
    for b in range(QB):
        te.wait_ge(S("cp", 0, b, 0), 1)
        o = off(0, b, 0)
        te.matmul(blk(T.yo, b), T.pt[:, o:o + 128], vv(rank), start=True, stop=True).then_inc(T.sem.pvo, 1)
    transposes(1, 0)
    for c in range(3):
        weighted(0, c, c == 0, False)
    transposes(1, 1)
    te.wait_ge(T.sem.oc, 1)
    own_share(0, True)
    weighted(1, 0, True, False)
    weighted(1, 1, False, False)
    own_share(1, False)
    weighted(1, 2, False, True)

    for b in range(QB):
        ve.wait_ge(S("st", 0, b), 1)
        ve.tensor_reduce(col(T.negm, b), st[0][b][:, 0:128], AxisListType.X, amax,
                         negate=True).then_inc(S("red", 0, b), 1)
    for b in range(QB):
        ve.wait_ge(S("red", 0, b), 1)
        ve.tensor_scalar(st[1][b][:, W1:W1 + 1], col(T.negm, b), -1.0, None, mult).then_inc(S("put", b), 1)
    for b in range(QB):
        ve.wait_ge(S("tr", 0, b, 0), 1)
        k = CHUNKS.index((0, b, 0))
        o = off(0, b, 0)
        ve.tensor_copy(T.pt[:, o:o + 128], tp[k % NT][:, 0:128]).then_inc(S("cp", 0, b, 0), 1)
    for b in range(QB):
        ve.wait_ge(S("st", 1, b), SIZES[1])
        ve.wait_ge(S("put", b), 1)
        ve.tensor_reduce(col(T.negm, QB + b), st[1][b][:, 0:W1 + 1], AxisListType.X, amax,
                         negate=True).then_inc(S("red", 1, b), 1)
    for c in range(SIZES[1]):
        ve.wait_ge(S("tr", 1, 0, c), 1)
        k = CHUNKS.index((1, 0, c))
        o = off(1, 0, c)
        ve.tensor_copy(T.pt[:, o:o + 128], tp[k % NT][:, 0:128]).then_inc(S("cp", 1, 0, c), 1)
    ve.wait_ge(T.sem.idn, 1)
    for b in range(QB):
        ve.wait_ge(S("f", b), 1)
        ve.tensor_scalar(blk(T.df, b), T.ident[:], col(T.fcol, b), None, mult).then_inc(S("df", b), 1)
        ne = len(EXC[1, b])
        for e in range(ne):
            ve.wait_ge(S("ex", 1, b, e), 1)
        if ne > 1:
            ve.tensor_reduce(col(T.ssum, b), T.lsum[:, lcol(1, b, 0):lcol(1, b, 0) + ne], AxisListType.X,
                             add).then_inc(S("ss", b), 1)
            ve.wait_ge(S("ss", b), 1)
            sums = col(T.ssum, b)
        else:
            sums = col(T.lsum, lcol(1, b, 0))
        ve.wait_ge(S("ex", 0, b, 0), 1)
        ve.tensor_scalar(col(T.lrun, b), col(T.lsum, lcol(0, b, 0)), col(T.fcol, b), sums,
                         mult, add).then_inc(S("l", b), 1)
    for b in range(QB):
        ve.wait_ge(S("l", b), 1)
    ve.reciprocal(T.rinv[:, 0:QB], T.lrun[:, 0:QB]).then_inc(T.sem.rc, 1)
    ve.wait_ge(T.sem.rc, 1)
    for b in range(QB):
        ve.wait_ge(S("pv", b), SIZES[1] + 1)
        ve.tensor_scalar(blk(T.ys, b), yp[b][:, 0:128], col(T.rinv, b), None, mult).then_inc(S("ny", b), 1)

    def exps(lv, b):
        ac.wait_ge(S("red", lv, b), 1)
        for e, (c0, c1) in enumerate(EXC[lv, b]):
            ac.activation(T.p[:, off(lv, b, c0):off(lv, b, c1)], st[lv][b][:, c0 * 128:c1 * 128], Exp,
                          bias=col(T.negm, lv * QB + b), scale=1.0,
                          accum_out=col(T.lsum, lcol(lv, b, e))).then_inc(S("ex", lv, b, e), 1)

    for b in range(QB):
        exps(0, b)
    for b in range(QB):
        exps(1, b)
        ac.activation(col(T.fcol, b), col(T.negm, b), Exp, bias=col(T.negm, QB + b),
                      scale=-1.0).then_inc(S("f", b), 1)
    ac.wait_ge(T.sem.pvo, QB)
    ac.activation(T.op[:, 0:QB * 128], T.yo[:, 0:QB * 128], Copy).then_inc(T.sem.oc, 1)
    for c in range(SIZES[1]):
        ac.wait_ge(S("tr", 1, 1, c), 1)
        k = CHUNKS.index((1, 1, c))
        o = off(1, 1, c)
        ac.activation(T.pt[:, o:o + 128], tp[k % NT][:, 0:128], Copy).then_inc(S("cp", 1, 1, c), 1)

    for b in range(QB):
        sy.wait_ge(S("ny", b), 1)
        sy.dma_start(T.y[b * 128:(b + 1) * 128, :], blk(T.ys, b)).then_inc(T.sem.out, 16)
    sy.wait_ge(T.sem.out, 16 * QB)
